import numpy as np
import ml_dtypes


def mxq(x, axis, fmt="e4m3"):
    dtype, down = {"e4m3": (ml_dtypes.float8_e4m3fn, 7), "e5m2": (ml_dtypes.float8_e5m2, 14)}[fmt]
    v = np.moveaxis(np.asarray(x, np.float32).astype(ml_dtypes.bfloat16).astype(np.float64), axis, -1)
    blocks = v.reshape(v.shape[:-1] + (-1, 32))
    amax = np.abs(blocks).max(-1, keepdims=True)
    byte = np.maximum(np.where(amax > 0, np.frexp(amax)[1] - 1 + 127, 0) - down, 1)
    scale = np.exp2(byte - 127.0)
    codes = (blocks / scale).astype(np.float32).astype(dtype).astype(np.float64)
    return np.moveaxis((codes * scale).reshape(v.shape), -1, axis)


WIDE = False


def mx_kscale(k):
    if not WIDE:
        return np.ones(k)
    levels = np.array([10, -10, 5, -5, 0])
    if k % 512:
        return np.exp2(np.random.permutation(np.resize(levels, k // 32))).repeat(32)
    a = np.empty((k // 512, 16))
    for p in range(k // 512):
        a[p, :8] = np.random.permutation(np.resize(levels, 8))
        for g in range(8):
            far = levels[np.abs(levels - a[p, g]) >= 10]
            a[p, g + 8] = far[np.random.randint(len(far))]
    return np.exp2(a.ravel()).repeat(32)


def f64(x):
    return np.asarray(x).astype(np.float64)


def striped(idx):
    return np.tile(np.asarray(idx).reshape(-1, 16).T, (8, 1)).astype(np.uint16)


def unstriped(offs):
    return offs[:16].T.reshape(-1).astype(np.int64)


E2M1 = np.array([0.0, 0.5, 1.0, 1.5, 2.0, 3.0, 4.0, 6.0, -0.0, -0.5, -1.0, -1.5, -2.0, -3.0, -4.0, -6.0])


def pack_weight(w, fmt):
    k, n = w.shape
    w = f64(np.asarray(w, np.float32).astype(ml_dtypes.bfloat16)).reshape(k // 32, 32, n)
    amax = np.abs(w).max(1)
    if fmt == "e4m3":
        byte = np.frexp(amax)[1] - 1 + 127 - 7
    else:
        mant, ex = np.frexp(amax / 6.0)
        byte = np.where(mant > 0.5, ex, ex - 1) + 127
    byte = np.clip(np.where(amax > 0, byte, 1), 1, 254)
    scaled = (w * np.exp2(127.0 - byte)[:, None, :]).reshape(k, n).astype(np.float32)
    by_word = np.ascontiguousarray(scaled.reshape(k // 512, 128, 4, n).transpose(0, 1, 3, 2))
    if fmt == "e4m3":
        words = by_word.astype(ml_dtypes.float8_e4m3fn).view(np.uint8)
    else:
        c = by_word.astype(ml_dtypes.float4_e2m1fn).view(np.uint8) & 0xF
        words = (c[..., 0::2] | (c[..., 1::2] << 4)).reshape(k // 512, 128, 2 * n)
    return np.ascontiguousarray(words), np.ascontiguousarray(byte.astype(np.uint8).reshape(k // 512, 16, n))


def unpack_weight(words, scales, fmt):
    g, _, n = scales.shape
    words = np.ascontiguousarray(words).reshape(g, 128, n, -1)
    if fmt == "e4m3":
        vals = words.view(ml_dtypes.float8_e4m3fn).astype(np.float64)
    else:
        nib = np.empty((g, 128, n, 4), np.uint8)
        nib[..., 0::2] = words & 0xF
        nib[..., 1::2] = words >> 4
        vals = E2M1[nib]
    vals = vals * np.repeat(np.exp2(scales.astype(np.float64) - 127.0), 8, axis=1)[..., None]
    return vals.transpose(0, 1, 3, 2).reshape(g * 512, n)


K, Q, I, C, J, N = 512, 128, 256, 512, 256, 256


def setup_inputs():
    n = np.random.standard_normal
    idx = np.random.permutation(C)[:I]
    idx2 = np.random.permutation(C)[:I]
    idx3 = np.random.permutation(C)[:J]
    idx4 = np.random.permutation(C)[:J]
    fk = mx_kscale(K)
    wp = pack_weight(n((K, N)) * 1 / np.sqrt(K) / fk[:, None], "e4m3")
    return {
        "ca": (np.random.randint(-7, 8, (Q, I)).astype(np.float64)).astype(np.float32),
        "ga": (np.random.uniform(0.1, 0.4, (Q, 1)) * fk[::4, None]).astype(np.float32),
        "cb": (np.random.randint(-7, 8, (Q, I)).astype(np.float64)).astype(np.float32),
        "gb": (np.random.uniform(0.1, 0.4, (Q, 1)) * fk[::4, None]).astype(np.float32),
        "cc": (np.random.randint(-7, 8, (Q, I)).astype(np.float64)).astype(np.float32),
        "gc": (np.random.uniform(0.1, 0.4, (Q, 1)) * fk[::4, None]).astype(np.float32),
        "cd": (np.random.randint(-7, 8, (Q, I)).astype(np.float64)).astype(np.float32),
        "gd": (np.random.uniform(0.1, 0.4, (Q, 1)) * fk[::4, None]).astype(np.float32),
        "w_words": wp[0],
        "w_scales": wp[1],
        "offs": striped(idx),
        "offs2": striped(idx2),
        "offs3": striped(idx3),
        "offs4": striped(idx4),
    }


def reference(ca, ga, cb, gb, cc, gc, cd, gd, w_words, w_scales, offs, offs2, offs3, offs4):
    idx = unstriped(offs)
    idx2 = unstriped(offs2)
    idx3 = unstriped(offs3)
    idx4 = unstriped(offs4)
    wu = unpack_weight(w_words, w_scales, "e4m3")
    p0 = np.zeros((Q, C))
    p0[:, idx] = f64(ca) * f64(ga)
    p1 = np.zeros((Q, C))
    p1[:, idx] = f64(cb) * f64(gb)
    p2 = np.zeros((Q, C))
    p2[:, idx2] = f64(cc) * f64(gc)
    p3 = np.zeros((Q, C))
    p3[:, idx2] = f64(cd) * f64(gd)
    v0 = p0[:, idx3]
    v1 = p1[:, idx4]
    v2 = p2[:, idx3]
    v3 = p3[:, idx4]
    z = np.stack([v0, v1, v2, v3], axis=1).reshape(K, J)
    zq = mxq(z, 0, "e4m3")
    p = wu.T @ zq
    return p

from contextlib import ExitStack

import concourse.mybir as mybir

F32 = mybir.dt.float32
BF16 = mybir.dt.bfloat16
I32 = mybir.dt.int32
U32 = mybir.dt.uint32
U16 = mybir.dt.uint16
U8 = mybir.dt.uint8
FP8X4 = mybir.dt.float8_e4m3fn_x4
COPY = mybir.ActivationFunctionType.Copy

P = 128
PACK = 4
CODES = 256
PAGE = 512
CASES = 256
N = 256
LIST_COLS = CODES // 16
FLOPS = 2 * 512 * N * CASES
CHUNKS = [[0,128],[128,256]]
ORDER = [["get",0,0,256],["get",1,0,256],["get",2,0,128],["get",3,0,128],["fin",0],["get",2,128,256],["get",3,128,256],["fin",1]]


def tile_list_fourpages_kernel(tc, ca, ga, cb, gb, cc, gc, cd, gd, w_words, w_scales, offs, offs2, offs3, offs4, out):
    nc = tc.nc
    with ExitStack() as ctx:
        keep = ctx.enter_context(tc.tile_pool(name="keep", bufs=1))
        psum = ctx.enter_context(tc.psum_pool(name="psum", bufs=1))

        lists = [keep.tile([P, LIST_COLS], U16, name="list%d" % t) for t in range(4)]
        codes = [keep.tile([P, CODES], F32, align_bytes=64, name="codes%d" % t, tag="codes%d" % t) for t in range(4)]
        steps = [keep.tile([P, 1], F32, name="steps%d" % t) for t in range(4)]
        pages = [keep.tile([P, PAGE], F32, name="page%d" % t) for t in range(4)]
        w_tile = keep.tile([P, N], U32, align_bytes=64)
        w_plane = keep.tile([P, N], U8, align_bytes=64)
        warm_in = keep.tile([P, 1], F32)
        warm_out = keep.tile([P, 1], F32)
        nc.vector.memset(warm_in[:], 0.0)
        nc.scalar.activation(warm_out[:], warm_in[:], COPY)

        for t in range(4):
            nc.vector.memset(pages[t][:], 0.0)
        nc.vector.memset(w_plane[:].bitcast(U32), 0)

        nc.scalar.dma_start(steps[0][:], ga)
        nc.sync.dma_start(codes[0][:], ca)
        nc.sync.dma_start(lists[0][:], offs)
        nc.sync.dma_start(steps[1][:], gb)
        nc.sync.dma_start(codes[1][:], cb)
        nc.sync.dma_start(steps[2][:], gc)
        nc.sync.dma_start(codes[2][:], cc)
        nc.sync.dma_start(steps[3][:], gd)
        nc.sync.dma_start(codes[3][:], cd)
        nc.sync.dma_start(lists[2][:], offs3)
        nc.sync.dma_start(lists[3][:], offs4)
        nc.sync.dma_start(lists[1][:], offs2)
        nc.sync.dma_start(w_tile[:].bitcast(I32), w_words[0].rearrange("p n t -> p (n t)").bitcast(I32))
        for q in range(4):
            nc.sync.dma_start(w_plane[32 * q : 32 * q + 4, :].bitcast(I32), w_scales[0, 4 * q : 4 * q + 4, :].bitcast(I32))

        put_list = [lists[0], lists[0], lists[1], lists[1]]
        get_list = [lists[2], lists[3], lists[2], lists[3]]

        def put(t):
            nc.scalar.activation(pages[t][:].indirect(put_list[t][:]), codes[t][:], COPY, scale=steps[t][:])

        def fetch(t, lo, hi):
            nc.scalar.activation(
                z[:, PACK * lo + t : PACK * hi : PACK],
                pages[t][:].indirect(get_list[t][:, lo // 16 : hi // 16]),
                COPY,
            )

        out_rows = out.rearrange("(h p) j -> p h j", p=P)

        def finish(i):
            lo, hi = CHUNKS[i]
            width = hi - lo
            z_words = keep.tile([P, width], U32, align_bytes=64, name="z_words%d" % i)
            z_plane = keep.tile([P, width], U8, align_bytes=64, name="z_plane%d" % i)
            nc.vector.quantize_mx(out=z_words[:].bitcast(FP8X4), scales=z_plane[:], in_=z[:, PACK * lo : PACK * hi])
            last = i == len(CHUNKS) - 1
            if last and True:
                for h in range(2):
                    acc = psum.tile([P, width], F32, name="acc%d_%d" % (i, h))
                    res = keep.tile([P, width], F32, name="res%d_%d" % (i, h))
                    cols = slice(h * P, (h + 1) * P)
                    nc.tensor.matmul_mx(out=acc[:], lhsT=w_tile[:, cols].bitcast(FP8X4), lhsT_scale=w_plane[:, cols],
                                        rhs=z_words[:].bitcast(FP8X4), rhs_scale=z_plane[:], start=True, stop=True)
                    if h == 0:
                        nc.vector.tensor_copy(res[:], acc[:])
                        nc.sync.dma_start(out[cols, lo:hi], res[:])
                    else:
                        nc.scalar.copy(res[:], acc[:])
                        nc.scalar.dma_start(out[cols, lo:hi], res[:])
            else:
                acc = psum.tile([P, 2, width], F32, name="acc%d" % i)
                res = keep.tile([P, 2, width], F32, name="res%d" % i)
                for h in range(2):
                    cols = slice(h * P, (h + 1) * P)
                    nc.tensor.matmul_mx(out=acc[:, h, :], lhsT=w_tile[:, cols].bitcast(FP8X4), lhsT_scale=w_plane[:, cols],
                                        rhs=z_words[:].bitcast(FP8X4), rhs_scale=z_plane[:], start=True, stop=True)
                nc.vector.tensor_copy(res[:], acc[:])
                nc.sync.dma_start(out_rows[:, :, lo:hi], res[:])

        for t in range(4):
            put(t)
        z = keep.tile([P, PACK * CASES], BF16, align_bytes=64, tag="codes2")
        for step in ORDER:
            if step[0] == "put":
                put(step[1])
            elif step[0] == "get":
                fetch(step[1], step[2], step[3])
            else:
                finish(step[1])
